import numpy as np
import ml_dtypes


def mxq(x, axis, fmt="e4m3"):
    dtype, down = {"e4m3": (ml_dtypes.float8_e4m3fn, 7), "e5m2": (ml_dtypes.float8_e5m2, 14)}[fmt]
    v = np.moveaxis(np.asarray(x, np.float32).astype(ml_dtypes.bfloat16).astype(np.float64), axis, -1)
    blocks = v.reshape(v.shape[:-1] + (-1, 32))
    amax = np.abs(blocks).max(-1, keepdims=True)
    byte = np.maximum(np.where(amax > 0, np.frexp(amax)[1] - 1 + 127, 0) - down, 1)
    scale = np.exp2(byte - 127.0)
    codes = (blocks / scale).astype(np.float32).astype(dtype).astype(np.float64)
    return np.moveaxis((codes * scale).reshape(v.shape), -1, axis)


WIDE = False


def mx_kscale(k):
    if not WIDE:
        return np.ones(k)
    levels = np.array([10, -10, 5, -5, 0])
    if k % 512:
        return np.exp2(np.random.permutation(np.resize(levels, k // 32))).repeat(32)
    a = np.empty((k // 512, 16))
    for p in range(k // 512):
        a[p, :8] = np.random.permutation(np.resize(levels, 8))
        for g in range(8):
            far = levels[np.abs(levels - a[p, g]) >= 10]
            a[p, g + 8] = far[np.random.randint(len(far))]
    return np.exp2(a.ravel()).repeat(32)


def f64(x):
    return np.asarray(x).astype(np.float64)


def striped(idx):
    return np.tile(np.asarray(idx).reshape(-1, 16).T, (8, 1)).astype(np.uint16)


def unstriped(offs):
    return offs[:16].T.reshape(-1).astype(np.int64)


B, N, T, D, DV, NQ = 2, 512, 2048, 512, 256, 256
PAGE = 64


def setup_inputs():
    n = np.random.standard_normal
    pages = np.random.permutation(T // PAGE)[:B * N // PAGE]
    idx = (pages[:, None] * PAGE + np.arange(PAGE)[None, :]).reshape(-1)
    s = mx_kscale(D)[:, None]
    u = np.ones(T)
    u[idx] = mx_kscale(B * N)
    r = np.random.uniform(0.5, 2.0, T)
    k = n((D, T)) / s
    v = n((DV, T)) / (u * r)
    return {
        "qT": (n((B, D, NQ)) * s * (1.00 / np.sqrt(D))).astype(np.float32),
        "kT": k.astype(np.float32),
        "vT": v.astype(np.float32),
        "vs": np.tile(u * r, (128, 1)).astype(np.float32),
        "kb": np.tile(n(T), (128, 1)).astype(np.float32),
        "offs": striped(idx),
    }


def reference(qT, kT, vT, vs, kb, offs):
    idx = unstriped(offs)
    k = f64(kT)
    v = f64(vT)
    pick = lambda x: x[:, idx].reshape(x.shape[0], B, N).transpose(1, 0, 2)
    q = f64(qT)
    score = mxq(q, 1, "e4m3").transpose(0, 2, 1) @ mxq(pick(k), 1, "e4m3")
    score = score + pick(f64(kb))[:, :1, :]
    p = 1.0 / (1.0 + np.exp(-score))
    w = p * pick(f64(vs))[:, :1, :]
    y = mxq(w, 2, "e4m3") @ mxq(pick(v).transpose(0, 2, 1), 1, "e4m3")
    y = y / 16.0
    return y

from contextlib import ExitStack

import concourse.mybir as mybir
from concourse.masks import make_identity

B, NQ, D, DV, N, T = 2, 256, 512, 256, 512, 2048
P = 128
PACK = 4
FLOPS = 2 * B * NQ * N * (D + DV)
BYTES = 4 * (B * D * NQ + D * T + DV * T + 2 * T + B * NQ * DV) + 2 * P * (B * N // 16)

F32 = mybir.dt.float32
BF16 = mybir.dt.bfloat16
U32 = mybir.dt.uint32
I32 = mybir.dt.int32
U16 = mybir.dt.uint16
U8 = mybir.dt.uint8
FP8X4 = mybir.dt.float8_e4m3fn_x4
COPY = mybir.ActivationFunctionType.Copy
SIGMOID = mybir.ActivationFunctionType.Sigmoid
MULT = mybir.AluOpType.mult

CHUNKS = (((0, 1024, 640), (1024, 1024, 640)), ((0, 1024, 640), (1024, 1024, 384)))


def tile_attend_sigmoid_kernel(tc, qT, kT, vT, vs, kb, offs, out):
    nc = tc.nc
    with ExitStack() as ctx:
        keep = ctx.enter_context(tc.tile_pool(name="keep", bufs=1))
        psum_s = ctx.enter_context(tc.psum_pool(name="psum_s", bufs=4))
        psum_t = ctx.enter_context(tc.psum_pool(name="psum_t", bufs=2))
        psum_y = ctx.enter_context(tc.psum_pool(name="psum_y", bufs=2))

        lists = keep.tile([P, B * N // 16], U16, name="lists")
        nc.sync.dma_start(lists[:], offs)

        k_rows = kT.rearrange("(p j) n -> p j n", j=PACK)
        staged = {}
        for c in range(2):
            for h, (n0, width, _) in enumerate(CHUNKS[c]):
                raw = keep.tile([P, 2, width], F32, name=f"k_raw{c}{h}")
                nc.sync.dma_start(out=raw[:], in_=k_rows[:, 2 * c : 2 * c + 2, n0 : n0 + width])
                staged[c, h] = raw
        q_rows = qT.rearrange("b (p j) q -> b p j q", j=PACK)
        q_raw = []
        for b in range(B):
            raw = keep.tile([P, PACK, NQ], F32, name=f"q_raw{b}")
            nc.sync.dma_start(out=raw[:], in_=q_rows[b])
            q_raw.append(raw)
        v_rows = vT.rearrange("(e p) n -> e p n", p=P)
        v_win = []
        for e in range(2):
            win = keep.tile([P, T], F32, name=f"v_win{e}")
            nc.sync.dma_start(out=win[:], in_=v_rows[e])
            v_win.append(win)

        warm = keep.tile([P, 1], F32, name="warm")
        nc.vector.memset(warm[:], 0.0)
        warmed = keep.tile([P, 1], F32, name="warmed")
        nc.scalar.activation(warmed[:], warm[:], SIGMOID)

        kb_win = keep.tile([P, T], F32, name="kb_win")
        vs_win = keep.tile([P, T], F32, name="vs_win")
        nc.vector.memset(kb_win[:], 0.0)
        nc.vector.memset(vs_win[:], 0.0)
        nc.scalar.dma_start(out=kb_win[0:1, :], in_=kb[0:1, :])
        nc.scalar.dma_start(out=vs_win[0:1, :], in_=vs[0:1, :])
        ident = keep.tile([P, P], F32, name="ident")
        make_identity(nc, ident[:])

        cols = []
        for name, win in (("kb", kb_win), ("vs", vs_win)):
            got = keep.tile([P, B * N], F32, name=f"{name}_got")
            nc.vector.tensor_copy(got[:], win[:].indirect(lists[:]))
            col = keep.tile([P, B, PACK], F32, name=f"{name}_col")
            for b in range(B):
                turned = psum_t.tile([P, PACK, P], F32, name="turned")
                for t in range(PACK):
                    nc.tensor.transpose(turned[:, t, :], got[:, b * N + t : (b + 1) * N : PACK], ident[:])
                nc.vector.tensor_copy(col[:, b, :], turned[:, :, 0])
            cols.append(col)
        kb_col, vs_col = cols

        words = []
        for b in range(B):
            got = keep.tile([P, 2 * 2 * N], BF16, name=f"k_got{b}", align_bytes=64)
            words.append(got)
        for c in range(2):
            pool_words = keep.tile([P, 2 * T], BF16, name=f"k_pool{c}", align_bytes=64)
            for h, (n0, width, split) in enumerate(CHUNKS[c]):
                raw = staged[c, h]
                dst = pool_words[:, 2 * n0 : 2 * (n0 + width)].rearrange("p (c i e) -> p c e i", i=4, e=2)
                src = raw[:].rearrange("p e (c i) -> p c e i", i=4)
                g = split // 4
                nc.scalar.activation(dst[:, :g], src[:, :g], COPY)
                nc.vector.tensor_copy(dst[:, g:], src[:, g:])
            for b in range(B):
                nc.vector.tensor_copy(
                    words[b][:].bitcast(U32)[:, c * N : (c + 1) * N],
                    pool_words[:].bitcast(U32).indirect(lists[:, b * (N // 16) : (b + 1) * (N // 16)]),
                )

        q_codes = keep.tile([P, B * NQ], U32, name="q_codes", align_bytes=64)
        q_scales = keep.tile([P, B * NQ], U8, name="q_scales", align_bytes=64)
        for b in range(B):
            grouped = keep.tile([P, NQ * PACK], BF16, name=f"q_grouped{b}", align_bytes=64)
            nc.scalar.activation(
                grouped[:].rearrange("p (c i j) -> p c j i", i=4, j=PACK),
                q_raw[b][:].rearrange("p j (c i) -> p c j i", i=4),
                COPY,
            )
            span = slice(b * NQ, (b + 1) * NQ)
            nc.vector.quantize_mx(out=q_codes[:, span].bitcast(FP8X4), scales=q_scales[:, span], in_=grouped[:])

        p_tiles = []
        for b in range(B):
            grouped = keep.tile([P, N * PACK], BF16, name=f"k_grouped{b}", align_bytes=64)
            nc.vector.tensor_copy(
                grouped[:].bitcast(I32).rearrange("p (t s c) -> p s c t", t=PACK, c=2),
                words[b][:].bitcast(I32).rearrange("p (c s t) -> p s c t", t=PACK, c=2),
            )
            k_codes = keep.tile([P, N], U32, name=f"k_codes{b}", align_bytes=64)
            k_scales = keep.tile([P, N], U8, name=f"k_scales{b}", align_bytes=64)
            nc.vector.quantize_mx(out=k_codes[:].bitcast(FP8X4), scales=k_scales[:], in_=grouped[:])
            prob = keep.tile([P, PACK, NQ], F32, name=f"prob{b}")
            span = slice(b * NQ, (b + 1) * NQ)
            for half in range(2):
                score = psum_s.tile([P, 2, NQ], F32, name="score")
                for u in range(2):
                    t = 2 * half + u
                    cols_t = slice(t * P, (t + 1) * P)
                    nc.tensor.matmul_mx(
                        out=score[:, u, :],
                        lhsT=k_codes[:, cols_t].bitcast(FP8X4),
                        lhsT_scale=k_scales[:, cols_t],
                        rhs=q_codes[:, span].bitcast(FP8X4),
                        rhs_scale=q_scales[:, span],
                        start=True,
                        stop=True,
                    )
                for u in range(2):
                    t = 2 * half + u
                    nc.scalar.activation(prob[:, t, :], score[:, u, :], SIGMOID, bias=kb_col[:, b, t : t + 1])
            p_tiles.append(prob)

        w_codes, w_scales = [], []
        for b in range(B):
            grouped = keep.tile([P, NQ * PACK], BF16, name=f"w_grouped{b}", align_bytes=64)
            nc.vector.tensor_tensor(
                grouped[:].rearrange("p (c i t) -> p c t i", i=4, t=PACK),
                p_tiles[b][:].rearrange("p t (c i) -> p c t i", i=4),
                vs_col[:, b, :].unsqueeze(1).unsqueeze(3).to_broadcast([P, NQ // 4, PACK, 4]),
                MULT,
            )
            codes = keep.tile([P, NQ], U32, name=f"w_codes{b}", align_bytes=64)
            scales = keep.tile([P, NQ], U8, name=f"w_scales{b}", align_bytes=64)
            nc.vector.quantize_mx(out=codes[:].bitcast(FP8X4), scales=scales[:], in_=grouped[:])
            w_codes.append(codes)
            w_scales.append(scales)

        for e in range(2):
            for b in range(B):
                got = keep.tile([P, N], F32, name=f"v_got{e}{b}")
                nc.vector.tensor_copy(got[:], v_win[e][:].indirect(lists[:, b * (N // 16) : (b + 1) * (N // 16)]))
                turned = psum_t.tile([P, PACK, P], F32, name="turned")
                for t in range(PACK):
                    nc.tensor.transpose(turned[:, t, :], got[:, t :: PACK], ident[:])
                grouped = keep.tile([P, P * PACK], BF16, name=f"v_grouped{e}{b}", align_bytes=64)
                nc.scalar.activation(
                    grouped[:].rearrange("p (e t) -> p e t", t=PACK), turned[:].rearrange("p t e -> p e t"), COPY
                )
                v_codes = keep.tile([P, P], U32, name=f"v_codes{e}{b}", align_bytes=64)
                v_scales = keep.tile([P, P], U8, name=f"v_scales{e}{b}", align_bytes=64)
                nc.vector.quantize_mx(out=v_codes[:].bitcast(FP8X4), scales=v_scales[:], in_=grouped[:])
                y = psum_y.tile([P, 2, P], F32, name="y")
                for h in range(2):
                    rows = slice(h * P, (h + 1) * P)
                    nc.tensor.matmul_mx(
                        out=y[:, h, :],
                        lhsT=w_codes[b][:, rows].bitcast(FP8X4),
                        lhsT_scale=w_scales[b][:, rows],
                        rhs=v_codes[:].bitcast(FP8X4),
                        rhs_scale=v_scales[:],
                        start=True,
                        stop=True,
                    )
                result = keep.tile([P, 2, P], F32, name=f"result{e}{b}")
                nc.scalar.activation(result[:], y[:], COPY, scale=1.0 / 16.0)
                nc.sync.dma_start(
                    out=out[b].rearrange("(h p) e -> p h e", p=P)[:, :, e * P : (e + 1) * P], in_=result[:]
                )
